import numpy as np
import ml_dtypes


def mxq(x, axis, fmt="e4m3"):
    dtype, down = {"e4m3": (ml_dtypes.float8_e4m3fn, 7), "e5m2": (ml_dtypes.float8_e5m2, 14)}[fmt]
    v = np.moveaxis(np.asarray(x, np.float32).astype(ml_dtypes.bfloat16).astype(np.float64), axis, -1)
    blocks = v.reshape(v.shape[:-1] + (-1, 32))
    amax = np.abs(blocks).max(-1, keepdims=True)
    byte = np.maximum(np.where(amax > 0, np.frexp(amax)[1] - 1 + 127, 0) - down, 1)
    scale = np.exp2(byte - 127.0)
    codes = (blocks / scale).astype(np.float32).astype(dtype).astype(np.float64)
    return np.moveaxis((codes * scale).reshape(v.shape), -1, axis)


WIDE = False


def mx_kscale(k):
    if not WIDE:
        return np.ones(k)
    levels = np.array([10, -10, 5, -5, 0])
    if k % 512:
        return np.exp2(np.random.permutation(np.resize(levels, k // 32))).repeat(32)
    a = np.empty((k // 512, 16))
    for p in range(k // 512):
        a[p, :8] = np.random.permutation(np.resize(levels, 8))
        for g in range(8):
            far = levels[np.abs(levels - a[p, g]) >= 10]
            a[p, g + 8] = far[np.random.randint(len(far))]
    return np.exp2(a.ravel()).repeat(32)


def f64(x):
    return np.asarray(x).astype(np.float64)


def striped(idx):
    return np.tile(idx.reshape(-1, 16).T, (8, 1)).astype(np.uint16)


def unstriped(offs):
    return offs[:16].T.reshape(-1).astype(np.int64)


def relu(v):
    return np.maximum(v, 0.0)


def d_relu(v):
    return (v > 0).astype(np.float64)


K, T, E, C, H, N = 384, 768, 6, 128, 512, 1024


def by_expert(wq, xq):
    return np.concatenate([wq[e].T @ xq[:, e * C:(e + 1) * C] for e in range(E)], axis=1)


def setup_inputs():
    n = np.random.standard_normal
    s = mx_kscale(N)[:, None]
    u = mx_kscale(H)
    return {
        "dyT": (n((N, T)) * s).astype(np.float32),
        "a1": n((H, E * C)).astype(np.float32),
        "a3": n((H, E * C)).astype(np.float32),
        "w2": (n((E, N, H)) / np.sqrt(N) / s[None] * u[None, None, :]).astype(np.float32),
        "w1": (n((E, H, K)) / np.sqrt(H) / u[None, :, None]).astype(np.float32),
        "w3": (n((E, H, K)) / np.sqrt(H) / u[None, :, None]).astype(np.float32),
        "gate": np.tile(np.random.uniform(0.2, 1.0, E * C), (N, 1)).astype(np.float32),
        "offs": striped(np.random.permutation(T)[:E * C]),
    }


def reference(dyT, a1, a3, w2, w1, w3, gate, offs):
    idx = unstriped(offs)
    gq = mxq(f64(gate) * f64(dyT)[:, idx], 0, "e4m3")
    dh = by_expert(mxq(f64(w2), 1, "e4m3"), gq)
    da1 = dh * f64(a3) * d_relu(f64(a1))
    da3 = dh * relu(f64(a1))
    dx = by_expert(mxq(f64(w1), 1, "e4m3"), mxq(da1, 0, "e4m3")) + by_expert(mxq(f64(w3), 1, "e4m3"), mxq(da3, 0, "e4m3"))
    out = np.zeros((K, T))
    out[:, idx] = dx
    return out

@@ -1,0 +1,250 @@
+from contextlib import ExitStack
+
+import concourse.mybir as mybir
+
+K, T, E, C, H, N = 384, 768, 6, 128, 512, 1024
+FLOPS = 2 * E * C * (N * H + 2 * H * K)
+BYTES = 4 * (N * T + 2 * H * E * C + E * N * H + 2 * E * H * K + E * C + K * T) + 2 * 128 * E * C // 16
+
+F32 = mybir.dt.float32
+BF16 = mybir.dt.bfloat16
+U32 = mybir.dt.uint32
+U16 = mybir.dt.uint16
+U8 = mybir.dt.uint8
+FP8X4 = mybir.dt.float8_e4m3fn_x4
+MULT = mybir.AluOpType.mult
+MAX = mybir.AluOpType.max
+GT = mybir.AluOpType.is_gt
+
+P = 128
+KB = K // P
+CHUNKS = ((0, 256), (256, 512))
+LOADS = "gate dy00 w2_00 dy01 dy02 dy03 w2_01 dy10 dy11 dy12 dy13 w2_10 a1 w2_11 a3 w13_00 w13_01 w2_20 w2_21 w13_10 w13_11 w2_30 w2_31 w13_20 w13_21 w2_40 w2_41 w13_30 w13_31 w2_50 w2_51 w13_40 w13_41 w13_50a w13_51a w13_50b w13_51b"
+ORDER = "G0 G1 W0 W1 H0 H1 U02 D0 X0 F0 W2 U22 D1 H2 X1 F1 W3 D2 H3 X2 F2 W4 U42 D3 H4 X3 F3 W5 D4 H5 X4 F4 D5 X5 F5"
+V2 = ((2, 0), (5, 1))
+V13 = ((1, 1, 0), (4, 1, 0), (5, 1, 256))
+
+
+def tile_moe_bdx_glu_relu_kernel(tc, dyT, a1, a3, w2, w1, w3, gate, offs, out):
+    nc = tc.nc
+    with ExitStack() as ctx:
+        keep = ctx.enter_context(tc.tile_pool(name="keep", bufs=1))
+        raw2p = ctx.enter_context(tc.tile_pool(name="raw2p", bufs=6))
+        raw13p = ctx.enter_context(tc.tile_pool(name="raw13p", bufs=5))
+        w2ip = ctx.enter_context(tc.tile_pool(name="w2ip", bufs=3))
+        w2p = ctx.enter_context(tc.tile_pool(name="w2p", bufs=6))
+        w13ip = ctx.enter_context(tc.tile_pool(name="w13ip", bufs=2))
+        w13p = ctx.enter_context(tc.tile_pool(name="w13p", bufs=3))
+        gp = ctx.enter_context(tc.tile_pool(name="gp", bufs=2))
+        dap = ctx.enter_context(tc.tile_pool(name="dap", bufs=3))
+        psum_h = ctx.enter_context(tc.psum_pool(name="psum_h", bufs=4))
+        psum_x = ctx.enter_context(tc.psum_pool(name="psum_x", bufs=4))
+
+        idx = keep.tile([P, E * C // 16], U16, name="idx")
+        nc.sync.dma_start(idx[:], offs)
+
+        w2v = w2.rearrange("e (c p j) i -> e c p j i", c=2, j=4)
+        w1v = w1.rearrange("e (p j) k -> e p j k", j=4)
+        w3v = w3.rearrange("e (p j) k -> e p j k", j=4)
+        dyv = dyT.rearrange("(c p t) w -> c p t w", c=2, t=4)
+        gate_t = keep.tile([P, E * C], F32, name="gate_t")
+        a1t = keep.tile([P, 4, E * C], F32, name="a1t")
+        a3t = keep.tile([P, 4, E * C], F32, name="a3t")
+
+        raw2 = {}
+        raw13 = {}
+        dy = {}
+
+        def load(what):
+            if what == "gate":
+                nc.sync.dma_start(out=gate_t[:], in_=gate[0:P, :])
+            elif what == "gateA":
+                nc.sync.dma_start(out=gate_t[:, 0:256], in_=gate[0:P, 0:256])
+            elif what == "gateB":
+                nc.sync.dma_start(out=gate_t[:, 256:768], in_=gate[0:P, 256:768])
+            elif what == "a1":
+                nc.sync.dma_start(out=a1t[:], in_=a1.rearrange("(p t) s -> p t s", t=4))
+            elif what == "a3":
+                nc.sync.dma_start(out=a3t[:], in_=a3.rearrange("(p t) s -> p t s", t=4))
+            elif what.startswith("dy"):
+                c, t = int(what[2]), int(what[3])
+                d = keep.tile([P, T], F32, name=f"dy{c}{t}")
+                nc.sync.dma_start(out=d[:], in_=dyv[c, :, t, :])
+                dy[c, t] = d
+            elif what.startswith("w2"):
+                e, c = int(what[3]), int(what[4])
+                raw = raw2p.tile([P, 4, H], F32, name="raw2")
+                nc.sync.dma_start(out=raw[:], in_=w2v[e, c])
+                raw2[e, c] = raw
+            else:
+                e, m = int(what[4]), int(what[5])
+                view = (w1v, w3v)[m][e]
+                part = what[6:]
+                if part in ("", "a"):
+                    raw = raw13p.tile([P, 4, K], F32, name="raw13")
+                    raw13[e, m] = raw
+                raw = raw13[e, m]
+                if part == "":
+                    nc.sync.dma_start(out=raw[:], in_=view)
+                elif part == "a":
+                    nc.sync.dma_start(out=raw[:, :, 0:256], in_=view[:, :, 0:256])
+                else:
+                    nc.sync.dma_start(out=raw[:, :, 256:384], in_=view[:, :, 256:384])
+
+        for what in LOADS.split():
+            load(what)
+        outs = []
+        for b in range(KB):
+            o = keep.tile([P, T], F32, name=f"out{b}")
+            outs.append(o)
+
+        gq = {}
+
+        def gather(h):
+            s0, n = CHUNKS[h]
+            for c in range(2):
+                gf = gp.tile([P, 4, n], F32, name="gf")
+                for t in range(4):
+                    nc.vector.tensor_tensor(
+                        gf[:, t, :], dy[c, t][:].indirect(idx[:, s0 // 16 : (s0 + n) // 16]), gate_t[:, s0 : s0 + n], MULT
+                    )
+                gi = gp.tile([P, n * 4], BF16, name="gi", align_bytes=64)
+                nc.scalar.copy(
+                    out=gi[:].rearrange("p (g i t) -> p g t i", i=4, t=4),
+                    in_=gf[:].rearrange("p t (g i) -> p g t i", i=4),
+                )
+                codes = keep.tile([P, n], U32, name=f"gcodes{h}{c}", align_bytes=64)
+                scales = keep.tile([P, n], U8, name=f"gscales{h}{c}", align_bytes=64)
+                nc.vector.quantize_mx(out=codes[:].bitcast(FP8X4), scales=scales[:], in_=gi[:])
+                gq[h, c] = (codes, scales)
+
+        q2 = {}
+
+        def weights2(e):
+            for c in range(2):
+                wi = w2ip.tile([P, H * 4], BF16, name="w2i", align_bytes=64)
+                src = raw2[e, c][:].rearrange("p j (m t) -> p m j t", t=4)
+                dst = wi[:].rearrange("p (t m j) -> p m j t", t=4, j=4)
+                if (e, c) in V2:
+                    nc.vector.tensor_copy(out=dst, in_=src)
+                else:
+                    nc.scalar.copy(out=dst, in_=src)
+                codes = w2p.tile([P, H], U32, name="w2codes", align_bytes=64)
+                scales = w2p.tile([P, H], U8, name="w2scales", align_bytes=64)
+                nc.vector.quantize_mx(out=codes[:].bitcast(FP8X4), scales=scales[:], in_=wi[:])
+                q2[e, c] = (codes, scales)
+
+        def columns(e, m, b):
+            if e < E - 1:
+                return m * K + b * P
+            return m * 2 * P + b * P if b < 2 else (4 + m) * P
+
+        q13 = {}
+
+        def weights13(e):
+            wi = w13ip.tile([P, 2 * K, 4], BF16, name="w13i", align_bytes=64)
+            codes = w13p.tile([P, 2 * K], U32, name="w13codes", align_bytes=64)
+            scales = w13p.tile([P, 2 * K], U8, name="w13scales", align_bytes=64)
+            parts = ((0, K),) if e < E - 1 else ((0, 2 * P), (2 * P, P))
+            for k0, n in parts:
+                for m in range(2):
+                    at = columns(e, m, k0 // P)
+                    dst = wi[:, at : at + n, :].rearrange("p (g i) j -> p g j i", i=4)
+                    src = raw13[e, m][:, :, k0 : k0 + n].rearrange("p j (g i) -> p g j i", i=4)
+                    if (e, m, k0) in V13:
+                        nc.vector.tensor_copy(out=dst, in_=src)
+                    else:
+                        nc.scalar.copy(out=dst, in_=src)
+            flat = wi[:].rearrange("p k j -> p (k j)")
+            for lo, hi in ((0, 512), (512, 768)):
+                nc.vector.quantize_mx(
+                    out=codes[:, lo:hi].bitcast(FP8X4), scales=scales[:, lo:hi], in_=flat[:, 4 * lo : 4 * hi]
+                )
+            q13[e] = (codes, scales)
+
+        dhs = {}
+
+        def hidden(e):
+            h = 0 if e * C < CHUNKS[0][1] else 1
+            s0 = e * C - CHUNKS[h][0]
+            dh = psum_h.tile([P, 4, C], F32, name="dh")
+            for t in range(4):
+                for c in range(2):
+                    wc, ws = q2[e, c]
+                    gc, gs = gq[h, c]
+                    nc.tensor.matmul_mx(
+                        out=dh[:, t, :],
+                        lhsT=wc[:, t * P : (t + 1) * P].bitcast(FP8X4),
+                        lhsT_scale=ws[:, t * P : (t + 1) * P],
+                        rhs=gc[:, s0 : s0 + C].bitcast(FP8X4),
+                        rhs_scale=gs[:, s0 : s0 + C],
+                        start=(c == 0),
+                        stop=(c == 1),
+                    )
+            dhs[e] = dh
+
+        def mask(e, n):
+            slots = slice(e * C, (e + n) * C)
+            nc.vector.scalar_tensor_tensor(
+                out=a3t[:, :, slots], in0=a1t[:, :, slots], scalar=0.0, in1=a3t[:, :, slots], op0=GT, op1=MULT
+            )
+
+        qda = {}
+
+        def gradient(e):
+            slots = slice(e * C, (e + 1) * C)
+            da = dap.tile([P, 2, C, 4], BF16, name="da", align_bytes=64)
+            dhv = dhs[e][:].rearrange("p t j -> p j t")
+            nc.vector.tensor_tensor(da[:, 0], dhv, a3t[:, :, slots].rearrange("p t j -> p j t"), MULT)
+            nc.vector.scalar_tensor_tensor(
+                out=da[:, 1], in0=a1t[:, :, slots].rearrange("p t j -> p j t"), scalar=0.0, in1=dhv, op0=MAX, op1=MULT
+            )
+            codes = dap.tile([P, 2 * C], U32, name="dacodes", align_bytes=64)
+            scales = dap.tile([P, 2 * C], U8, name="dascales", align_bytes=64)
+            nc.vector.quantize_mx(
+                out=codes[:].bitcast(FP8X4), scales=scales[:], in_=da[:].rearrange("p m j t -> p (m j t)")
+            )
+            qda[e] = (codes, scales)
+
+        def finish(e):
+            codes, scales = qda[e]
+            wc, ws = q13[e]
+            dx = psum_x.tile([P, KB, C], F32, name="dx")
+            dxs = dap.tile([P, KB, C], F32, name="dxs")
+            for b in range(KB):
+                for m in range(2):
+                    at = columns(e, m, b)
+                    nc.tensor.matmul_mx(
+                        out=dx[:, b, :],
+                        lhsT=wc[:, at : at + P].bitcast(FP8X4),
+                        lhsT_scale=ws[:, at : at + P],
+                        rhs=codes[:, m * C : (m + 1) * C].bitcast(FP8X4),
+                        rhs_scale=scales[:, m * C : (m + 1) * C],
+                        start=(m == 0),
+                        stop=(m == 1),
+                    )
+            if e < E - 1:
+                nc.scalar.copy(out=dxs[:], in_=dx[:])
+            for b in range(KB):
+                if e == E - 1:
+                    nc.scalar.copy(out=dxs[:, b, :], in_=dx[:, b, :])
+                nc.vector.tensor_copy(outs[b][:].indirect(idx[:, e * 8 : (e + 1) * 8]), dxs[:, b, :])
+
+        for step in ORDER.split():
+            kind, e = step[0], int(step[1])
+            if kind == "G":
+                gather(e)
+            elif kind == "W":
+                weights2(e)
+            elif kind == "X":
+                weights13(e)
+            elif kind == "H":
+                hidden(e)
+            elif kind == "U":
+                mask(e, int(step[2]))
+            elif kind == "D":
+                gradient(e)
+            else:
+                finish(e)
+        for b in range(KB):
+            nc.sync.dma_start(out=out[b * P : (b + 1) * P, :], in_=outs[b][:])

@@ -19,10 +19,25 @@ GT = mybir.AluOpType.is_gt
 P = 128
 KB = K // P
 CHUNKS = ((0, 256), (256, 512))
-LOADS = "gate dy00 w2_00 dy01 dy02 dy03 w2_01 dy10 dy11 dy12 dy13 w2_10 a1 w2_11 a3 w13_00 w13_01 w2_20 w2_21 w13_10 w13_11 w2_30 w2_31 w13_20 w13_21 w2_40 w2_41 w13_30 w13_31 w2_50 w2_51 w13_40 w13_41 w13_50a w13_51a w13_50b w13_51b"
-ORDER = "G0 G1 W0 W1 H0 H1 U02 D0 X0 F0 W2 U22 D1 H2 X1 F1 W3 D2 H3 X2 F2 W4 U42 D3 H4 X3 F3 W5 D4 H5 X4 F4 D5 X5 F5"
-V2 = ((2, 0), (5, 1))
-V13 = ((1, 1, 0), (4, 1, 0), (5, 1, 256))
+ORDER = """
+gate,0,768 dy,0,0 w2,0,0 G,0,0,0 dy,0,1 dy,0,2 dy,0,3 i2,0,0 w2,0,1 G,0,0,1 G,1,0,1 G,0,0,2 dy,1,0
+G,0,0,3 dy,1,1 G,1,0,2 gi,0,0 dy,1,2 dy,1,3 G,1,0,3 i2,0,1 w2,1,0 qg,0,0 G,0,1,0 G,0,1,1 a1 G,0,1,2
+G,0,1,3 G,1,0,0 gi,0,1 G,1,1,1 i2,1,0 w2,1,1 qg,0,1 G,1,1,0 gi,1,0 a3 G,1,1,2 G,1,1,3 qg,1,0 gi,1,1
+w13,0,0,0,384 q2,0,0 q2,0,1 q2,1,0 w13,0,1,0,384 mh,0 i2,1,1 qg,1,1 u,0,2 w2,2,0 i13,0,0,0,384 A,0
+q2,1,1 B,0 w2,2,1 mh,1 i13,0,1,0,384 u,2,2 qd,0 i2,2,0 w13,1,0,0,384 q13,0,0 q13,0,1 A,1 mx,0,0
+mx,0,1 w13,1,1,0,384 mx,0,2 B,1 i2,2,1 q2,2,0 qd,1 w2,3,0 u,4,2 c,0,0,3 i13,1,0,0,384 q2,2,1 s,0,0
+w2,3,1 mh,2 s,0,1 i2,3,0 s,0,2 w13,2,0,0,384 i13,1,1,0,384,V A,2 w13,2,1,0,384 i2,3,1 q13,1,0
+q13,1,1 q2,3,0 w2,4,0 mx,1,0 mx,1,1 mx,1,2 B,2 i13,2,0,0,384 q2,3,1 qd,2 mh,3 w2,4,1 c,1,0,3
+i13,2,1,0,384,V s,1,0 i2,4,0 s,1,1 w13,3,0,0,384 s,1,2 w13,3,1,0,384 q13,2,0 i2,4,1 q13,2,1 q2,4,0
+mx,2,0 mx,2,1 w2,5,0 mx,2,2 A,3 c,2,0,3 q2,4,1 i13,3,0,0,384 s,2,0 mh,4 w2,5,1 s,2,1 s,2,2 i2,5,0
+B,3 w13,4,0,0,384 i13,3,1,0,384,V qd,3 w13,4,1,0,384 i2,5,1 q13,3,0 q13,3,1 q2,5,0 mx,3,0
+w13,5,0,0,256 mx,3,1 mx,3,2 A,4 i13,4,0,0,384 w13,5,1,0,256 q2,5,1 B,4 mh,5 w13,5,0,256,128 c,3,0,3
+i13,4,1,0,384,V w13,5,1,256,128 i13,5,0,0,256 s,3,0 i13,5,1,0,256 s,3,1 i13,5,0,256,128 s,3,2 qd,4
+q13,4,0 q13,4,1 A,5 mx,4,0 mx,4,1 mx,4,2 B,5 c,4,0,3 q13,5,0 s,4,0 s,4,1 s,4,2 qd,5
+i13,5,1,256,128,V mx,5,0 mx,5,1 q13,5,1 c,5,0,1 c,5,1,2 s,5,0 mx,5,2 c,5,2,3 s,5,1 st,0 s,5,2 st,1
+st,2
+
+"""
 
 
 def tile_moe_bdx_glu_relu_kernel(tc, dyT, a1, a3, w2, w1, w3, gate, offs, out):
@@ -44,207 +59,198 @@ def tile_moe_bdx_glu_relu_kernel(tc, dyT, a1, a3, w2, w1, w3, gate, offs, out):
         nc.sync.dma_start(idx[:], offs)
 
         w2v = w2.rearrange("e (c p j) i -> e c p j i", c=2, j=4)
-        w1v = w1.rearrange("e (p j) k -> e p j k", j=4)
-        w3v = w3.rearrange("e (p j) k -> e p j k", j=4)
+        w13v = (w1.rearrange("e (p j) k -> e p j k", j=4), w3.rearrange("e (p j) k -> e p j k", j=4))
         dyv = dyT.rearrange("(c p t) w -> c p t w", c=2, t=4)
         gate_t = keep.tile([P, E * C], F32, name="gate_t")
         a1t = keep.tile([P, 4, E * C], F32, name="a1t")
         a3t = keep.tile([P, 4, E * C], F32, name="a3t")
-
-        raw2 = {}
-        raw13 = {}
-        dy = {}
-
-        def load(what):
-            if what == "gate":
-                nc.sync.dma_start(out=gate_t[:], in_=gate[0:P, :])
-            elif what == "gateA":
-                nc.sync.dma_start(out=gate_t[:, 0:256], in_=gate[0:P, 0:256])
-            elif what == "gateB":
-                nc.sync.dma_start(out=gate_t[:, 256:768], in_=gate[0:P, 256:768])
-            elif what == "a1":
-                nc.sync.dma_start(out=a1t[:], in_=a1.rearrange("(p t) s -> p t s", t=4))
-            elif what == "a3":
-                nc.sync.dma_start(out=a3t[:], in_=a3.rearrange("(p t) s -> p t s", t=4))
-            elif what.startswith("dy"):
-                c, t = int(what[2]), int(what[3])
-                d = keep.tile([P, T], F32, name=f"dy{c}{t}")
-                nc.sync.dma_start(out=d[:], in_=dyv[c, :, t, :])
-                dy[c, t] = d
-            elif what.startswith("w2"):
-                e, c = int(what[3]), int(what[4])
-                raw = raw2p.tile([P, 4, H], F32, name="raw2")
-                nc.sync.dma_start(out=raw[:], in_=w2v[e, c])
-                raw2[e, c] = raw
-            else:
-                e, m = int(what[4]), int(what[5])
-                view = (w1v, w3v)[m][e]
-                part = what[6:]
-                if part in ("", "a"):
-                    raw = raw13p.tile([P, 4, K], F32, name="raw13")
-                    raw13[e, m] = raw
-                raw = raw13[e, m]
-                if part == "":
-                    nc.sync.dma_start(out=raw[:], in_=view)
-                elif part == "a":
-                    nc.sync.dma_start(out=raw[:, :, 0:256], in_=view[:, :, 0:256])
-                else:
-                    nc.sync.dma_start(out=raw[:, :, 256:384], in_=view[:, :, 256:384])
-
-        for what in LOADS.split():
-            load(what)
         outs = []
         for b in range(KB):
             o = keep.tile([P, T], F32, name=f"out{b}")
             outs.append(o)
+        tiles = {}
 
-        gq = {}
-
-        def gather(h):
-            s0, n = CHUNKS[h]
-            for c in range(2):
-                gf = gp.tile([P, 4, n], F32, name="gf")
-                for t in range(4):
-                    nc.vector.tensor_tensor(
-                        gf[:, t, :], dy[c, t][:].indirect(idx[:, s0 // 16 : (s0 + n) // 16]), gate_t[:, s0 : s0 + n], MULT
-                    )
-                gi = gp.tile([P, n * 4], BF16, name="gi", align_bytes=64)
-                nc.scalar.copy(
-                    out=gi[:].rearrange("p (g i t) -> p g t i", i=4, t=4),
-                    in_=gf[:].rearrange("p t (g i) -> p g t i", i=4),
-                )
-                codes = keep.tile([P, n], U32, name=f"gcodes{h}{c}", align_bytes=64)
-                scales = keep.tile([P, n], U8, name=f"gscales{h}{c}", align_bytes=64)
-                nc.vector.quantize_mx(out=codes[:].bitcast(FP8X4), scales=scales[:], in_=gi[:])
-                gq[h, c] = (codes, scales)
-
-        q2 = {}
-
-        def weights2(e):
-            for c in range(2):
-                wi = w2ip.tile([P, H * 4], BF16, name="w2i", align_bytes=64)
-                src = raw2[e, c][:].rearrange("p j (m t) -> p m j t", t=4)
-                dst = wi[:].rearrange("p (t m j) -> p m j t", t=4, j=4)
-                if (e, c) in V2:
-                    nc.vector.tensor_copy(out=dst, in_=src)
+        def get(pool, key, name, shape, dtype, align=64):
+            if key not in tiles:
+                if align:
+                    tiles[key] = pool.tile(shape, dtype, name=name, align_bytes=align)
                 else:
-                    nc.scalar.copy(out=dst, in_=src)
-                codes = w2p.tile([P, H], U32, name="w2codes", align_bytes=64)
-                scales = w2p.tile([P, H], U8, name="w2scales", align_bytes=64)
-                nc.vector.quantize_mx(out=codes[:].bitcast(FP8X4), scales=scales[:], in_=wi[:])
-                q2[e, c] = (codes, scales)
+                    tiles[key] = pool.tile(shape, dtype, name=name)
+            return tiles[key]
+
+        def chunk_of(e):
+            for h, (s0, n) in enumerate(CHUNKS):
+                if s0 <= e * C < s0 + n:
+                    return h
 
         def columns(e, m, b):
             if e < E - 1:
                 return m * K + b * P
             return m * 2 * P + b * P if b < 2 else (4 + m) * P
 
-        q13 = {}
+        def copy(eng, out, in_):
+            if eng == "V":
+                nc.vector.tensor_copy(out=out, in_=in_)
+            elif eng == "P":
+                nc.gpsimd.tensor_scalar(out, in_, 1.0, 0.0, MULT, mybir.AluOpType.add)
+            else:
+                nc.scalar.copy(out=out, in_=in_)
 
-        def weights13(e):
-            wi = w13ip.tile([P, 2 * K, 4], BF16, name="w13i", align_bytes=64)
-            codes = w13p.tile([P, 2 * K], U32, name="w13codes", align_bytes=64)
-            scales = w13p.tile([P, 2 * K], U8, name="w13scales", align_bytes=64)
-            parts = ((0, K),) if e < E - 1 else ((0, 2 * P), (2 * P, P))
-            for k0, n in parts:
-                for m in range(2):
-                    at = columns(e, m, k0 // P)
-                    dst = wi[:, at : at + n, :].rearrange("p (g i) j -> p g j i", i=4)
-                    src = raw13[e, m][:, :, k0 : k0 + n].rearrange("p j (g i) -> p g j i", i=4)
-                    if (e, m, k0) in V13:
-                        nc.vector.tensor_copy(out=dst, in_=src)
-                    else:
-                        nc.scalar.copy(out=dst, in_=src)
-            flat = wi[:].rearrange("p k j -> p (k j)")
-            for lo, hi in ((0, 512), (512, 768)):
-                nc.vector.quantize_mx(
-                    out=codes[:, lo:hi].bitcast(FP8X4), scales=scales[:, lo:hi], in_=flat[:, 4 * lo : 4 * hi]
+        def quantize(codes, scales, values):
+            nc.vector.quantize_mx(out=codes.bitcast(FP8X4), scales=scales, in_=values)
+
+        def do(kind, a, eng):
+            if kind == "gate":
+                nc.sync.dma_start(out=gate_t[:, a[0] : a[1]], in_=gate[0:P, a[0] : a[1]])
+            elif kind == "a1":
+                nc.sync.dma_start(out=a1t[:], in_=a1.rearrange("(p t) s -> p t s", t=4))
+            elif kind == "a3":
+                nc.sync.dma_start(out=a3t[:], in_=a3.rearrange("(p t) s -> p t s", t=4))
+            elif kind == "dy":
+                c, t = a
+                d = get(keep, ("dy", c, t), f"dy{c}{t}", [P, T], F32)
+                nc.sync.dma_start(out=d[:], in_=dyv[c, :, t, :])
+            elif kind == "w2":
+                e, c = a[0:2]
+                raw = get(raw2p, ("raw2", e, c), "raw2", [P, 4, H], F32)
+                i0, n = (0, H) if len(a) == 2 else a[2:4]
+                nc.sync.dma_start(out=raw[:, :, i0 : i0 + n], in_=w2v[e, c, :, :, i0 : i0 + n])
+            elif kind == "w13":
+                e, m, k0, n = a
+                raw = get(raw13p, ("raw13", e, m), "raw13", [P, 4, K], F32)
+                nc.sync.dma_start(out=raw[:, :, k0 : k0 + n], in_=w13v[m][e, :, :, k0 : k0 + n])
+            elif kind == "G":
+                h, c, t = a
+                s0, n = CHUNKS[h]
+                gf = get(gp, ("gf", h, c), "gf", [P, 4, n], F32)
+                nc.vector.tensor_tensor(
+                    gf[:, t, :],
+                    tiles["dy", c, t][:].indirect(idx[:, s0 // 16 : (s0 + n) // 16]),
+                    gate_t[:, s0 : s0 + n],
+                    MULT,
                 )
-            q13[e] = (codes, scales)
-
-        dhs = {}
-
-        def hidden(e):
-            h = 0 if e * C < CHUNKS[0][1] else 1
-            s0 = e * C - CHUNKS[h][0]
-            dh = psum_h.tile([P, 4, C], F32, name="dh")
-            for t in range(4):
-                for c in range(2):
-                    wc, ws = q2[e, c]
-                    gc, gs = gq[h, c]
-                    nc.tensor.matmul_mx(
-                        out=dh[:, t, :],
-                        lhsT=wc[:, t * P : (t + 1) * P].bitcast(FP8X4),
-                        lhsT_scale=ws[:, t * P : (t + 1) * P],
-                        rhs=gc[:, s0 : s0 + C].bitcast(FP8X4),
-                        rhs_scale=gs[:, s0 : s0 + C],
-                        start=(c == 0),
-                        stop=(c == 1),
+            elif kind == "gi":
+                h, c = a
+                n = CHUNKS[h][1]
+                gi = get(gp, ("gi", h, c), "gi", [P, n * 4], BF16)
+                copy(
+                    eng,
+                    gi[:].rearrange("p (g i t) -> p g t i", i=4, t=4),
+                    tiles["gf", h, c][:].rearrange("p t (g i) -> p g t i", i=4),
+                )
+            elif kind == "qg":
+                h, c = a
+                n = CHUNKS[h][1]
+                codes = get(keep, ("gc", h, c), f"gcodes{h}{c}", [P, n], U32)
+                scales = get(keep, ("gs", h, c), f"gscales{h}{c}", [P, n], U8)
+                quantize(codes[:], scales[:], tiles["gi", h, c][:])
+            elif kind == "i2":
+                e, c = a[0:2]
+                i0, n = (0, H) if len(a) == 2 else a[2:4]
+                wi = get(w2ip, ("w2i", e, c), "w2i", [P, 4, P, 4], BF16)
+                copy(
+                    eng,
+                    wi[:, :, i0 // 4 : (i0 + n) // 4, :].rearrange("p t m j -> p m t j"),
+                    tiles["raw2", e, c][:, :, i0 : i0 + n].rearrange("p j (m t) -> p m t j", t=4),
+                )
+            elif kind == "q2":
+                e, c = a
+                codes = get(w2p, ("w2c", e, c), "w2codes", [P, H], U32)
+                scales = get(w2p, ("w2s", e, c), "w2scales", [P, H], U8)
+                quantize(codes[:], scales[:], tiles["w2i", e, c][:].rearrange("p t m j -> p (t m j)"))
+            elif kind == "i13":
+                e, m, k0, n = a
+                wi = get(w13ip, ("w13i", e), "w13i", [P, 2 * K, 4], BF16)
+                at = columns(e, m, k0 // P)
+                copy(
+                    eng,
+                    wi[:, at : at + n, :].rearrange("p (g i) j -> p g j i", i=4),
+                    tiles["raw13", e, m][:, :, k0 : k0 + n].rearrange("p j (g i) -> p g j i", i=4),
+                )
+            elif kind == "q13":
+                e, part = a
+                codes = get(w13p, ("w13c", e), "w13codes", [P, 2 * K], U32)
+                scales = get(w13p, ("w13s", e), "w13scales", [P, 2 * K], U8)
+                flat = tiles["w13i", e][:].rearrange("p k j -> p (k j)")
+                lo, hi = ((0, 512), (512, 768))[part]
+                quantize(codes[:, lo:hi], scales[:, lo:hi], flat[:, 4 * lo : 4 * hi])
+            elif kind == "mh":
+                (e,) = a
+                h = chunk_of(e)
+                s0 = e * C - CHUNKS[h][0]
+                dh = get(psum_h, ("dh", e), "dh", [P, 4, C], F32, None)
+                for t in range(4):
+                    for c in range(2):
+                        nc.tensor.matmul_mx(
+                            out=dh[:, t, :],
+                            lhsT=tiles["w2c", e, c][:, t * P : (t + 1) * P].bitcast(FP8X4),
+                            lhsT_scale=tiles["w2s", e, c][:, t * P : (t + 1) * P],
+                            rhs=tiles["gc", h, c][:, s0 : s0 + C].bitcast(FP8X4),
+                            rhs_scale=tiles["gs", h, c][:, s0 : s0 + C],
+                            start=(c == 0),
+                            stop=(c == 1),
+                        )
+            elif kind == "u":
+                e, n = a
+                slots = slice(e * C, (e + n) * C)
+                nc.vector.scalar_tensor_tensor(
+                    out=a3t[:, :, slots], in0=a1t[:, :, slots], scalar=0.0, in1=a3t[:, :, slots], op0=GT, op1=MULT
+                )
+            elif kind in ("A", "B"):
+                (e,) = a
+                slots = slice(e * C, (e + 1) * C)
+                da = get(dap, ("da", e), "da", [P, 2, C, 4], BF16)
+                dhv = tiles["dh", e][:].rearrange("p t j -> p j t")
+                if kind == "B":
+                    nc.vector.tensor_tensor(da[:, 0], dhv, a3t[:, :, slots].rearrange("p t j -> p j t"), MULT)
+                else:
+                    nc.vector.scalar_tensor_tensor(
+                        out=da[:, 1],
+                        in0=a1t[:, :, slots].rearrange("p t j -> p j t"),
+                        scalar=0.0,
+                        in1=dhv,
+                        op0=MAX,
+                        op1=MULT,
                     )
-            dhs[e] = dh
-
-        def mask(e, n):
-            slots = slice(e * C, (e + n) * C)
-            nc.vector.scalar_tensor_tensor(
-                out=a3t[:, :, slots], in0=a1t[:, :, slots], scalar=0.0, in1=a3t[:, :, slots], op0=GT, op1=MULT
-            )
-
-        qda = {}
-
-        def gradient(e):
-            slots = slice(e * C, (e + 1) * C)
-            da = dap.tile([P, 2, C, 4], BF16, name="da", align_bytes=64)
-            dhv = dhs[e][:].rearrange("p t j -> p j t")
-            nc.vector.tensor_tensor(da[:, 0], dhv, a3t[:, :, slots].rearrange("p t j -> p j t"), MULT)
-            nc.vector.scalar_tensor_tensor(
-                out=da[:, 1], in0=a1t[:, :, slots].rearrange("p t j -> p j t"), scalar=0.0, in1=dhv, op0=MAX, op1=MULT
-            )
-            codes = dap.tile([P, 2 * C], U32, name="dacodes", align_bytes=64)
-            scales = dap.tile([P, 2 * C], U8, name="dascales", align_bytes=64)
-            nc.vector.quantize_mx(
-                out=codes[:].bitcast(FP8X4), scales=scales[:], in_=da[:].rearrange("p m j t -> p (m j t)")
-            )
-            qda[e] = (codes, scales)
-
-        def finish(e):
-            codes, scales = qda[e]
-            wc, ws = q13[e]
-            dx = psum_x.tile([P, KB, C], F32, name="dx")
-            dxs = dap.tile([P, KB, C], F32, name="dxs")
-            for b in range(KB):
+            elif kind == "qd":
+                (e,) = a
+                codes = get(dap, ("dc", e), "dacodes", [P, 2 * C], U32)
+                scales = get(dap, ("ds", e), "dascales", [P, 2 * C], U8)
+                quantize(codes[:], scales[:], tiles["da", e][:].rearrange("p m j t -> p (m j t)"))
+            elif kind == "mx":
+                e, b = a
+                dx = get(psum_x, ("dx", e), "dx", [P, KB, C], F32, None)
                 for m in range(2):
                     at = columns(e, m, b)
                     nc.tensor.matmul_mx(
                         out=dx[:, b, :],
-                        lhsT=wc[:, at : at + P].bitcast(FP8X4),
-                        lhsT_scale=ws[:, at : at + P],
-                        rhs=codes[:, m * C : (m + 1) * C].bitcast(FP8X4),
-                        rhs_scale=scales[:, m * C : (m + 1) * C],
+                        lhsT=tiles["w13c", e][:, at : at + P].bitcast(FP8X4),
+                        lhsT_scale=tiles["w13s", e][:, at : at + P],
+                        rhs=tiles["dc", e][:, m * C : (m + 1) * C].bitcast(FP8X4),
+                        rhs_scale=tiles["ds", e][:, m * C : (m + 1) * C],
                         start=(m == 0),
                         stop=(m == 1),
                     )
-            if e < E - 1:
-                nc.scalar.copy(out=dxs[:], in_=dx[:])
-            for b in range(KB):
-                if e == E - 1:
-                    nc.scalar.copy(out=dxs[:, b, :], in_=dx[:, b, :])
-                nc.vector.tensor_copy(outs[b][:].indirect(idx[:, e * 8 : (e + 1) * 8]), dxs[:, b, :])
+            elif kind == "c":
+                e, b0, b1 = a
+                dxs = get(dap, ("dxs", e), "dxs", [P, KB, C], F32)
+                nc.scalar.copy(out=dxs[:, b0:b1, :], in_=tiles["dx", e][:, b0:b1, :])
+            elif kind == "s":
+                e, b = a
+                nc.vector.tensor_copy(outs[b][:].indirect(idx[:, e * 8 : (e + 1) * 8]), tiles["dxs", e][:, b, :])
+            elif kind == "st":
+                (b,) = a
+                nc.sync.dma_start(out=out[b * P : (b + 1) * P, :], in_=outs[b][:])
+            else:
+                assert False, kind
 
         for step in ORDER.split():
-            kind, e = step[0], int(step[1])
-            if kind == "G":
-                gather(e)
-            elif kind == "W":
-                weights2(e)
-            elif kind == "X":
-                weights13(e)
-            elif kind == "H":
-                hidden(e)
-            elif kind == "U":
-                mask(e, int(step[2]))
-            elif kind == "D":
-                gradient(e)
-            else:
-                finish(e)
-        for b in range(KB):
-            nc.sync.dma_start(out=out[b * P : (b + 1) * P, :], in_=outs[b][:])
+            fields = step.split(",")
+            numbers = []
+            eng = "S"
+            for f in fields[1:]:
+                if f in ("V", "S", "P"):
+                    eng = f
+                else:
+                    numbers.append(int(f))
+            do(fields[0], tuple(numbers), eng)

from contextlib import ExitStack

import concourse.mybir as mybir

K, T, E, C, H, N = 384, 768, 6, 128, 512, 1024
FLOPS = 2 * E * C * (N * H + 2 * H * K)
BYTES = 4 * (N * T + 2 * H * E * C + E * N * H + 2 * E * H * K + E * C + K * T) + 2 * 128 * E * C // 16

F32 = mybir.dt.float32
BF16 = mybir.dt.bfloat16
U32 = mybir.dt.uint32
U16 = mybir.dt.uint16
U8 = mybir.dt.uint8
FP8X4 = mybir.dt.float8_e4m3fn_x4
MULT = mybir.AluOpType.mult
MAX = mybir.AluOpType.max
GT = mybir.AluOpType.is_gt

P = 128
KB = K // P
CHUNKS = ((0, 256), (256, 512))
ORDER = """
gate,0,768 dy,0,0 w2,0,0 G,0,0,0 dy,0,1 dy,0,2 dy,0,3 i2,0,0 w2,0,1 G,0,0,1 G,1,0,1 G,0,0,2 dy,1,0
G,0,0,3 dy,1,1 G,1,0,2 gi,0,0 dy,1,2 dy,1,3 G,1,0,3 i2,0,1 w2,1,0 qg,0,0 G,0,1,0 G,0,1,1 a1 G,0,1,2
G,0,1,3 G,1,0,0 gi,0,1 G,1,1,1 i2,1,0 w2,1,1 qg,0,1 G,1,1,0 gi,1,0 a3 G,1,1,2 G,1,1,3 qg,1,0 gi,1,1
w13,0,0,0,384 q2,0,0 q2,0,1 q2,1,0 w13,0,1,0,384 mh,0 i2,1,1 qg,1,1 u,0,2 w2,2,0 i13,0,0,0,384 A,0
q2,1,1 B,0 w2,2,1 mh,1 i13,0,1,0,384 u,2,2 qd,0 i2,2,0 w13,1,0,0,384 q13,0,0 q13,0,1 A,1 mx,0,0
mx,0,1 w13,1,1,0,384 mx,0,2 B,1 i2,2,1 q2,2,0 qd,1 w2,3,0 u,4,2 c,0,0,3 i13,1,0,0,384 q2,2,1 s,0,0
w2,3,1 mh,2 s,0,1 i2,3,0 s,0,2 w13,2,0,0,384 i13,1,1,0,384,V A,2 w13,2,1,0,384 i2,3,1 q13,1,0
q13,1,1 q2,3,0 w2,4,0 mx,1,0 mx,1,1 mx,1,2 B,2 i13,2,0,0,384 q2,3,1 qd,2 mh,3 w2,4,1 c,1,0,3
i13,2,1,0,384,V s,1,0 i2,4,0 s,1,1 w13,3,0,0,384 s,1,2 w13,3,1,0,384 q13,2,0 i2,4,1 q13,2,1 q2,4,0
mx,2,0 mx,2,1 w2,5,0 mx,2,2 A,3 c,2,0,3 q2,4,1 i13,3,0,0,384 s,2,0 mh,4 w2,5,1 s,2,1 s,2,2 i2,5,0
B,3 w13,4,0,0,384 i13,3,1,0,384,V qd,3 w13,4,1,0,384 i2,5,1 q13,3,0 q13,3,1 q2,5,0 mx,3,0
w13,5,0,0,256 mx,3,1 mx,3,2 A,4 i13,4,0,0,384 w13,5,1,0,256 q2,5,1 B,4 mh,5 w13,5,0,256,128 c,3,0,3
i13,4,1,0,384,V w13,5,1,256,128 i13,5,0,0,256 s,3,0 i13,5,1,0,256 s,3,1 i13,5,0,256,128 s,3,2 qd,4
q13,4,0 q13,4,1 A,5 mx,4,0 mx,4,1 mx,4,2 B,5 c,4,0,3 q13,5,0 s,4,0 s,4,1 s,4,2 qd,5
i13,5,1,256,128,V mx,5,0 mx,5,1 q13,5,1 c,5,0,1 c,5,1,2 s,5,0 mx,5,2 c,5,2,3 s,5,1 st,0 s,5,2 st,1
st,2

"""


def tile_moe_bdx_glu_relu_kernel(tc, dyT, a1, a3, w2, w1, w3, gate, offs, out):
    nc = tc.nc
    with ExitStack() as ctx:
        keep = ctx.enter_context(tc.tile_pool(name="keep", bufs=1))
        raw2p = ctx.enter_context(tc.tile_pool(name="raw2p", bufs=6))
        raw13p = ctx.enter_context(tc.tile_pool(name="raw13p", bufs=5))
        w2ip = ctx.enter_context(tc.tile_pool(name="w2ip", bufs=3))
        w2p = ctx.enter_context(tc.tile_pool(name="w2p", bufs=6))
        w13ip = ctx.enter_context(tc.tile_pool(name="w13ip", bufs=2))
        w13p = ctx.enter_context(tc.tile_pool(name="w13p", bufs=3))
        gp = ctx.enter_context(tc.tile_pool(name="gp", bufs=2))
        dap = ctx.enter_context(tc.tile_pool(name="dap", bufs=3))
        psum_h = ctx.enter_context(tc.psum_pool(name="psum_h", bufs=4))
        psum_x = ctx.enter_context(tc.psum_pool(name="psum_x", bufs=4))

        idx = keep.tile([P, E * C // 16], U16, name="idx")
        nc.sync.dma_start(idx[:], offs)

        w2v = w2.rearrange("e (c p j) i -> e c p j i", c=2, j=4)
        w13v = (w1.rearrange("e (p j) k -> e p j k", j=4), w3.rearrange("e (p j) k -> e p j k", j=4))
        dyv = dyT.rearrange("(c p t) w -> c p t w", c=2, t=4)
        gate_t = keep.tile([P, E * C], F32, name="gate_t")
        a1t = keep.tile([P, 4, E * C], F32, name="a1t")
        a3t = keep.tile([P, 4, E * C], F32, name="a3t")
        outs = []
        for b in range(KB):
            o = keep.tile([P, T], F32, name=f"out{b}")
            outs.append(o)
        tiles = {}

        def get(pool, key, name, shape, dtype, align=64):
            if key not in tiles:
                if align:
                    tiles[key] = pool.tile(shape, dtype, name=name, align_bytes=align)
                else:
                    tiles[key] = pool.tile(shape, dtype, name=name)
            return tiles[key]

        def chunk_of(e):
            for h, (s0, n) in enumerate(CHUNKS):
                if s0 <= e * C < s0 + n:
                    return h

        def columns(e, m, b):
            if e < E - 1:
                return m * K + b * P
            return m * 2 * P + b * P if b < 2 else (4 + m) * P

        def copy(eng, out, in_):
            if eng == "V":
                nc.vector.tensor_copy(out=out, in_=in_)
            elif eng == "P":
                nc.gpsimd.tensor_scalar(out, in_, 1.0, 0.0, MULT, mybir.AluOpType.add)
            else:
                nc.scalar.copy(out=out, in_=in_)

        def quantize(codes, scales, values):
            nc.vector.quantize_mx(out=codes.bitcast(FP8X4), scales=scales, in_=values)

        def do(kind, a, eng):
            if kind == "gate":
                nc.sync.dma_start(out=gate_t[:, a[0] : a[1]], in_=gate[0:P, a[0] : a[1]])
            elif kind == "a1":
                nc.sync.dma_start(out=a1t[:], in_=a1.rearrange("(p t) s -> p t s", t=4))
            elif kind == "a3":
                nc.sync.dma_start(out=a3t[:], in_=a3.rearrange("(p t) s -> p t s", t=4))
            elif kind == "dy":
                c, t = a
                d = get(keep, ("dy", c, t), f"dy{c}{t}", [P, T], F32)
                nc.sync.dma_start(out=d[:], in_=dyv[c, :, t, :])
            elif kind == "w2":
                e, c = a[0:2]
                raw = get(raw2p, ("raw2", e, c), "raw2", [P, 4, H], F32)
                i0, n = (0, H) if len(a) == 2 else a[2:4]
                nc.sync.dma_start(out=raw[:, :, i0 : i0 + n], in_=w2v[e, c, :, :, i0 : i0 + n])
            elif kind == "w13":
                e, m, k0, n = a
                raw = get(raw13p, ("raw13", e, m), "raw13", [P, 4, K], F32)
                nc.sync.dma_start(out=raw[:, :, k0 : k0 + n], in_=w13v[m][e, :, :, k0 : k0 + n])
            elif kind == "G":
                h, c, t = a
                s0, n = CHUNKS[h]
                gf = get(gp, ("gf", h, c), "gf", [P, 4, n], F32)
                nc.vector.tensor_tensor(
                    gf[:, t, :],
                    tiles["dy", c, t][:].indirect(idx[:, s0 // 16 : (s0 + n) // 16]),
                    gate_t[:, s0 : s0 + n],
                    MULT,
                )
            elif kind == "gi":
                h, c = a
                n = CHUNKS[h][1]
                gi = get(gp, ("gi", h, c), "gi", [P, n * 4], BF16)
                copy(
                    eng,
                    gi[:].rearrange("p (g i t) -> p g t i", i=4, t=4),
                    tiles["gf", h, c][:].rearrange("p t (g i) -> p g t i", i=4),
                )
            elif kind == "qg":
                h, c = a
                n = CHUNKS[h][1]
                codes = get(keep, ("gc", h, c), f"gcodes{h}{c}", [P, n], U32)
                scales = get(keep, ("gs", h, c), f"gscales{h}{c}", [P, n], U8)
                quantize(codes[:], scales[:], tiles["gi", h, c][:])
            elif kind == "i2":
                e, c = a[0:2]
                i0, n = (0, H) if len(a) == 2 else a[2:4]
                wi = get(w2ip, ("w2i", e, c), "w2i", [P, 4, P, 4], BF16)
                copy(
                    eng,
                    wi[:, :, i0 // 4 : (i0 + n) // 4, :].rearrange("p t m j -> p m t j"),
                    tiles["raw2", e, c][:, :, i0 : i0 + n].rearrange("p j (m t) -> p m t j", t=4),
                )
            elif kind == "q2":
                e, c = a
                codes = get(w2p, ("w2c", e, c), "w2codes", [P, H], U32)
                scales = get(w2p, ("w2s", e, c), "w2scales", [P, H], U8)
                quantize(codes[:], scales[:], tiles["w2i", e, c][:].rearrange("p t m j -> p (t m j)"))
            elif kind == "i13":
                e, m, k0, n = a
                wi = get(w13ip, ("w13i", e), "w13i", [P, 2 * K, 4], BF16)
                at = columns(e, m, k0 // P)
                copy(
                    eng,
                    wi[:, at : at + n, :].rearrange("p (g i) j -> p g j i", i=4),
                    tiles["raw13", e, m][:, :, k0 : k0 + n].rearrange("p j (g i) -> p g j i", i=4),
                )
            elif kind == "q13":
                e, part = a
                codes = get(w13p, ("w13c", e), "w13codes", [P, 2 * K], U32)
                scales = get(w13p, ("w13s", e), "w13scales", [P, 2 * K], U8)
                flat = tiles["w13i", e][:].rearrange("p k j -> p (k j)")
                lo, hi = ((0, 512), (512, 768))[part]
                quantize(codes[:, lo:hi], scales[:, lo:hi], flat[:, 4 * lo : 4 * hi])
            elif kind == "mh":
                (e,) = a
                h = chunk_of(e)
                s0 = e * C - CHUNKS[h][0]
                dh = get(psum_h, ("dh", e), "dh", [P, 4, C], F32, None)
                for t in range(4):
                    for c in range(2):
                        nc.tensor.matmul_mx(
                            out=dh[:, t, :],
                            lhsT=tiles["w2c", e, c][:, t * P : (t + 1) * P].bitcast(FP8X4),
                            lhsT_scale=tiles["w2s", e, c][:, t * P : (t + 1) * P],
                            rhs=tiles["gc", h, c][:, s0 : s0 + C].bitcast(FP8X4),
                            rhs_scale=tiles["gs", h, c][:, s0 : s0 + C],
                            start=(c == 0),
                            stop=(c == 1),
                        )
            elif kind == "u":
                e, n = a
                slots = slice(e * C, (e + n) * C)
                nc.vector.scalar_tensor_tensor(
                    out=a3t[:, :, slots], in0=a1t[:, :, slots], scalar=0.0, in1=a3t[:, :, slots], op0=GT, op1=MULT
                )
            elif kind in ("A", "B"):
                (e,) = a
                slots = slice(e * C, (e + 1) * C)
                da = get(dap, ("da", e), "da", [P, 2, C, 4], BF16)
                dhv = tiles["dh", e][:].rearrange("p t j -> p j t")
                if kind == "B":
                    nc.vector.tensor_tensor(da[:, 0], dhv, a3t[:, :, slots].rearrange("p t j -> p j t"), MULT)
                else:
                    nc.vector.scalar_tensor_tensor(
                        out=da[:, 1],
                        in0=a1t[:, :, slots].rearrange("p t j -> p j t"),
                        scalar=0.0,
                        in1=dhv,
                        op0=MAX,
                        op1=MULT,
                    )
            elif kind == "qd":
                (e,) = a
                codes = get(dap, ("dc", e), "dacodes", [P, 2 * C], U32)
                scales = get(dap, ("ds", e), "dascales", [P, 2 * C], U8)
                quantize(codes[:], scales[:], tiles["da", e][:].rearrange("p m j t -> p (m j t)"))
            elif kind == "mx":
                e, b = a
                dx = get(psum_x, ("dx", e), "dx", [P, KB, C], F32, None)
                for m in range(2):
                    at = columns(e, m, b)
                    nc.tensor.matmul_mx(
                        out=dx[:, b, :],
                        lhsT=tiles["w13c", e][:, at : at + P].bitcast(FP8X4),
                        lhsT_scale=tiles["w13s", e][:, at : at + P],
                        rhs=tiles["dc", e][:, m * C : (m + 1) * C].bitcast(FP8X4),
                        rhs_scale=tiles["ds", e][:, m * C : (m + 1) * C],
                        start=(m == 0),
                        stop=(m == 1),
                    )
            elif kind == "c":
                e, b0, b1 = a
                dxs = get(dap, ("dxs", e), "dxs", [P, KB, C], F32)
                nc.scalar.copy(out=dxs[:, b0:b1, :], in_=tiles["dx", e][:, b0:b1, :])
            elif kind == "s":
                e, b = a
                nc.vector.tensor_copy(outs[b][:].indirect(idx[:, e * 8 : (e + 1) * 8]), tiles["dxs", e][:, b, :])
            elif kind == "st":
                (b,) = a
                nc.sync.dma_start(out=out[b * P : (b + 1) * P, :], in_=outs[b][:])
            else:
                assert False, kind

        for step in ORDER.split():
            fields = step.split(",")
            numbers = []
            eng = "S"
            for f in fields[1:]:
                if f in ("V", "S", "P"):
                    eng = f
                else:
                    numbers.append(int(f))
            do(fields[0], tuple(numbers), eng)
